import numpy as np
import ml_dtypes


def mxq(x, axis, fmt="e4m3"):
    dtype, down = {"e4m3": (ml_dtypes.float8_e4m3fn, 7), "e5m2": (ml_dtypes.float8_e5m2, 14)}[fmt]
    v = np.moveaxis(np.asarray(x, np.float32).astype(ml_dtypes.bfloat16).astype(np.float64), axis, -1)
    blocks = v.reshape(v.shape[:-1] + (-1, 32))
    amax = np.abs(blocks).max(-1, keepdims=True)
    byte = np.maximum(np.where(amax > 0, np.frexp(amax)[1] - 1 + 127, 0) - down, 1)
    scale = np.exp2(byte - 127.0)
    codes = (blocks / scale).astype(np.float32).astype(dtype).astype(np.float64)
    return np.moveaxis((codes * scale).reshape(v.shape), -1, axis)


WIDE = False


def mx_kscale(k):
    if not WIDE:
        return np.ones(k)
    levels = np.array([24, -24, 12, -12, 0])
    if k % 512:
        return np.exp2(np.random.permutation(np.resize(levels, k // 32))).repeat(32)
    a = np.empty((k // 512, 16))
    for p in range(k // 512):
        a[p, :8] = np.random.permutation(np.resize(levels, 8))
        for g in range(8):
            far = levels[np.abs(levels - a[p, g]) >= 10]
            a[p, g + 8] = far[np.random.randint(len(far))]
    return np.exp2(a.ravel()).repeat(32)


def f64(x):
    return np.asarray(x).astype(np.float64)


def striped(idx):
    return np.tile(idx.reshape(-1, 16).T, (8, 1)).astype(np.uint16)


def unstriped(offs):
    return offs[:16].T.reshape(-1).astype(np.int64)


E2M1 = np.array([0.0, 0.5, 1.0, 1.5, 2.0, 3.0, 4.0, 6.0, -0.0, -0.5, -1.0, -1.5, -2.0, -3.0, -4.0, -6.0])


def pack_weight(w, fmt):
    k, n = w.shape
    w = f64(np.asarray(w, np.float32).astype(ml_dtypes.bfloat16)).reshape(k // 32, 32, n)
    amax = np.abs(w).max(1)
    if fmt == "e4m3":
        byte = np.frexp(amax)[1] - 1 + 127 - 7
    else:
        mant, ex = np.frexp(amax / 6.0)
        byte = np.where(mant > 0.5, ex, ex - 1) + 127
    byte = np.clip(np.where(amax > 0, byte, 1), 1, 254)
    scaled = (w * np.exp2(127.0 - byte)[:, None, :]).reshape(k, n).astype(np.float32)
    by_word = np.ascontiguousarray(scaled.reshape(k // 512, 128, 4, n).transpose(0, 1, 3, 2))
    if fmt == "e4m3":
        words = by_word.astype(ml_dtypes.float8_e4m3fn).view(np.uint8)
    else:
        c = by_word.astype(ml_dtypes.float4_e2m1fn).view(np.uint8) & 0xF
        words = (c[..., 0::2] | (c[..., 1::2] << 4)).reshape(k // 512, 128, 2 * n)
    return np.ascontiguousarray(words), np.ascontiguousarray(byte.astype(np.uint8).reshape(k // 512, 16, n))


def unpack_weight(words, scales, fmt):
    g, _, n = scales.shape
    words = np.ascontiguousarray(words).reshape(g, 128, n, -1)
    if fmt == "e4m3":
        vals = words.view(ml_dtypes.float8_e4m3fn).astype(np.float64)
    else:
        nib = np.empty((g, 128, n, 4), np.uint8)
        nib[..., 0::2] = words & 0xF
        nib[..., 1::2] = words >> 4
        vals = E2M1[nib]
    vals = vals * np.repeat(np.exp2(scales.astype(np.float64) - 127.0), 8, axis=1)[..., None]
    return vals.transpose(0, 1, 3, 2).reshape(g * 512, n)


def planes(y):
    n, m = y.shape
    v = y.astype(np.float32).astype(ml_dtypes.bfloat16).astype(np.float64).reshape(n // 32, 32, m)
    top = np.abs(v).max(1)
    byte = np.clip(np.where(top > 0, np.frexp(top)[1] - 1 + 127 - 7, 1), 1, 254)
    codes = (v * np.exp2(127.0 - byte)[:, None, :]).reshape(n, m).astype(np.float32).astype(ml_dtypes.float8_e4m3fn).view(np.uint8)
    words = codes.reshape(n // 512, 128, 4, m).transpose(0, 1, 3, 2)
    return np.ascontiguousarray(words), np.ascontiguousarray(byte.astype(np.uint8).reshape(n // 512, 16, m))


K, R, N, T, J = 512, 512, 512, 2048, 1024


def setup_inputs():
    n = np.random.standard_normal
    s = mx_kscale(K)[:, None]
    u = mx_kscale(R)[:, None]
    wb = 0.7 * n((K, N)) / np.sqrt(K) / s
    wb4 = pack_weight(wb, "e2m1")
    wbrest = wb - unpack_weight(*wb4, "e2m1")
    p_tab = pack_weight(n((K, T)) * s, "e4m3")
    p_wb8 = pack_weight(wbrest, "e4m3")
    p_dn = pack_weight(n((K, R)) / np.sqrt(K) / s * u.T, "e2m1")
    return {
        "tab_words": p_tab[0],
        "tab_scales": p_tab[1],
        "wb4_words": wb4[0],
        "wb4_scales": wb4[1],
        "wb8_words": p_wb8[0],
        "wb8_scales": p_wb8[1],
        "dn_words": p_dn[0],
        "dn_scales": p_dn[1],
        "upw": (2.0 * n((R, N)) / np.sqrt(R) / u).astype(np.float32),
        "x0T": (n((N, T))).astype(np.float32),
        "b": (0.3 * n(N)).astype(np.float32),
        "offs": striped(np.random.permutation(T)[:J]),
    }


def reference(tab_words, tab_scales, wb4_words, wb4_scales, wb8_words, wb8_scales, dn_words, dn_scales, upw, x0T, b, offs):
    idx = unstriped(offs)
    tab_ = unpack_weight(tab_words, tab_scales, "e4m3")[:, idx]
    wb4_ = unpack_weight(wb4_words, wb4_scales, "e2m1")
    wb8_ = unpack_weight(wb8_words, wb8_scales, "e4m3")
    dn_ = unpack_weight(dn_words, dn_scales, "e2m1")
    hs = dn_.T @ tab_
    h = hs
    h_ = mxq(h, 0, "e4m3")
    upw_ = mxq(f64(upw), 0, "e4m3")
    y = wb4_.T @ tab_ + wb8_.T @ tab_ + upw_.T @ h_
    out_0 = f64(x0T)[:, idx] * (y + f64(b)[:, None]) + f64(x0T)[:, idx]
    return (out_0,) + planes(out_0)

@@ -1,0 +1,201 @@
+from contextlib import ExitStack
+
+import concourse.mybir as mybir
+
+K, R, N, T, J = 512, 512, 512, 2048, 1024
+FLOPS = 2 * J * (K * R + 2 * K * N + R * N)
+
+F32 = mybir.dt.float32
+BF16 = mybir.dt.bfloat16
+I32 = mybir.dt.int32
+U32 = mybir.dt.uint32
+U16 = mybir.dt.uint16
+U8 = mybir.dt.uint8
+FP8X4 = mybir.dt.float8_e4m3fn_x4
+FP4X4 = mybir.dt.float4_e2m1fn_x4
+ALU = mybir.AluOpType
+ACT = mybir.ActivationFunctionType
+
+P = 128
+PACK = 4
+HALF = 512
+HALVES = J // HALF
+CH = 128
+QU = 256
+
+
+def tile_list_xcross_res_noneP_kernel(
+    tc, tab_words, tab_scales, wb4_words, wb4_scales, wb8_words, wb8_scales, dn_words, dn_scales, upw, x0T, b, offs,
+    out_0, out_1, out_2,
+):
+    nc = tc.nc
+    with ExitStack() as ctx:
+        keep = ctx.enter_context(tc.tile_pool(name="keep", bufs=1))
+        psum = ctx.enter_context(tc.psum_pool(name="psum", bufs=1))
+
+        def sb(shape, dtype, name, tag=""):
+            return keep.tile(shape, dtype, name=name, tag=tag or name, align_bytes=64)
+
+        def load(tile, src):
+            nc.sync.dma_start(out=tile.bitcast(I32), in_=src.bitcast(I32))
+
+        def load_scale_rows(queue, tile, rows):
+            for q in range(4):
+                queue.dma_start(out=tile[32 * q : 32 * q + 4, :].bitcast(I32), in_=rows[4 * q : 4 * q + 4, :].bitcast(I32))
+
+        offsets = keep.tile([P, J // 16], U16, name="offsets")
+
+        def entries(start, count):
+            return offsets[:, start // 16 : (start + count) // 16]
+
+        tab_s = sb([P, T], U8, "tab_s")
+        dn_s_raw = sb([P, R], U8, "dn_s_raw", "dn_s_raw_g_w1")
+        wb_s_raw = sb([P, 2 * N], U8, "wb_s_raw", "wb_s_raw_up_b")
+        wb_s_rows = sb([16, 2 * N], U8, "wb_s_rows")
+        nc.vector.memset(tab_s[:].bitcast(I32), 0)
+        nc.vector.memset(dn_s_raw[:].bitcast(I32), 0)
+        nc.vector.memset(wb_s_raw[:].bitcast(I32), 0)
+
+        tab_w = sb([P, T], U32, "tab_w")
+        dn_w_raw = sb([P, 2 * R], U8, "dn_w_raw")
+        up_raw = sb([P, PACK, N], F32, "up_raw", "up_raw_h_w0")
+        wb4_w_raw = sb([P, 2 * N], U8, "wb4_w_raw")
+        wb8_w_raw = sb([P, N], U32, "wb8_w_raw")
+        bias = sb([P, PACK], F32, "bias")
+        x_t = [sb([P, T], F32, f"x_{t}") for t in range(PACK)]
+        x_rows = x0T.rearrange("(p t) c -> p t c", t=PACK)
+
+        nc.gpsimd.dma_start(out=wb_s_rows[:, 0:N].bitcast(I32), in_=wb4_scales[0].bitcast(I32))
+        nc.gpsimd.dma_start(out=wb_s_rows[:, N:].bitcast(I32), in_=wb8_scales[0].bitcast(I32))
+        nc.gpsimd.dma_start(out=bias[:], in_=b.rearrange("(p t) -> p t", t=PACK))
+        bias1 = sb([P, PACK], F32, "bias1")
+        nc.gpsimd.tensor_scalar(bias1[:], bias[:], 1.0, 1.0, ALU.mult, ALU.add)
+
+        nc.sync.dma_start(offsets[:], offs)
+        load(dn_w_raw[:], dn_words[0])
+        load_scale_rows(nc.sync, tab_s, tab_scales[0])
+        load(tab_w[:], tab_words[0].rearrange("p t i -> p (t i)"))
+        load(wb4_w_raw[:], wb4_words[0])
+        load_scale_rows(nc.sync, dn_s_raw, dn_scales[0])
+        load(wb8_w_raw[:], wb8_words[0].rearrange("p n i -> p (n i)"))
+        nc.sync.dma_start(out=up_raw[:], in_=upw.rearrange("(p i) n -> p i n", i=PACK))
+        load_scale_rows(nc.sync, wb_s_raw, wb_s_rows)
+        for t in range(PACK):
+            nc.sync.dma_start(out=x_t[t][:], in_=x_rows[:, t, :])
+
+        g_s = [sb([P, HALF], U8, f"g_s{h}") for h in range(HALVES)]
+        for h in range(HALVES):
+            nc.vector.tensor_copy(g_s[h][:], tab_s[:].indirect(entries(h * HALF, HALF)))
+        g_w = [sb([P, HALF], U32, "g_w0")]
+        for c0 in range(0, HALF, QU):
+            nc.vector.tensor_copy(g_w[0][:, c0 : c0 + QU], tab_w[:].indirect(entries(c0, QU)))
+        dn_s = sb([P, R], U8, "dn_s")
+        nc.vector.tensor_copy(dn_s[:].rearrange("p (t m) -> p t m", t=PACK), dn_s_raw[:].rearrange("p (m t) -> p t m", t=PACK))
+        g_w.append(sb([P, HALF], U32, "g_w1", "dn_s_raw_g_w1"))
+        nc.vector.tensor_copy(g_w[1][:], tab_w[:].indirect(entries(HALF, HALF)))
+
+        def deal_words(dst, src):
+            nc.scalar.copy(dst.rearrange("p (t m) -> p t m", t=PACK), src.rearrange("p (m t) -> p t m", t=PACK))
+
+        dn_w = sb([P, 2 * R], U8, "dn_w")
+        deal_words(dn_w[:].bitcast(U16), dn_w_raw[:].bitcast(U16))
+        wb4_w = sb([P, 2 * N], U8, "wb4_w")
+        deal_words(wb4_w[:].bitcast(U16), wb4_w_raw[:].bitcast(U16))
+        wb8_w = sb([P, N], U32, "wb8_w")
+        deal_words(wb8_w[:], wb8_w_raw[:])
+
+        wb_s = sb([P, 2 * N], U8, "wb_s")
+        nc.vector.tensor_copy(
+            wb_s[:].rearrange("p (w t m) -> p w t m", w=2, t=PACK), wb_s_raw[:].rearrange("p (w m t) -> p w t m", w=2, t=PACK)
+        )
+        up_b = sb([P, PACK * N], BF16, "up_b", "wb_s_raw_up_b")
+        nc.vector.tensor_copy(
+            up_b[:].rearrange("p (t m i) -> p m i t", t=PACK, i=PACK), up_raw[:].rearrange("p i (m t) -> p m i t", t=PACK)
+        )
+        up_w = sb([P, N], U32, "up_w")
+        up_s = sb([P, N], U8, "up_s")
+        nc.vector.quantize_mx(out=up_w[:].bitcast(FP8X4), scales=up_s[:], in_=up_b[:])
+
+        h_w, h_s, y_sb = {}, {}, {}
+
+        def first_stage(h):
+            h_b = sb([P, HALF * PACK], BF16, f"h_b{h}")
+            for c in range(HALF // CH):
+                bank = psum.tile([P, PACK, CH], F32, name="h_bank", tag=f"bank{h * 4 + c}")
+                cols = slice(c * CH, (c + 1) * CH)
+                for t in range(PACK):
+                    nc.tensor.matmul_mx(
+                        out=bank[:, t, :],
+                        lhsT=dn_w[:, 2 * P * t : 2 * P * (t + 1)].bitcast(FP4X4), lhsT_scale=dn_s[:, P * t : P * (t + 1)],
+                        rhs=g_w[h][:, cols].bitcast(FP8X4), rhs_scale=g_s[h][:, cols],
+                        start=True, stop=True,
+                    )
+                nc.scalar.copy(
+                    h_b[:, c * CH * PACK : (c + 1) * CH * PACK].rearrange("p (j t) -> p j t", t=PACK),
+                    bank[:].rearrange("p t j -> p j t"),
+                )
+            h_w[h] = sb([P, HALF], U32, f"h_w{h}", "up_raw_h_w0" if h == 0 else "")
+            h_s[h] = sb([P, HALF], U8, f"h_s{h}")
+            nc.vector.quantize_mx(out=h_w[h][:].bitcast(FP8X4), scales=h_s[h][:], in_=h_b[:])
+
+        def second_stage(h, t):
+            bank = psum.tile([P, HALF], F32, name="y_bank", tag=f"bank{len(y_sb)}")
+            m = slice(P * t, P * (t + 1))
+            nc.tensor.matmul_mx(
+                out=bank[:], lhsT=wb4_w[:, 2 * P * t : 2 * P * (t + 1)].bitcast(FP4X4), lhsT_scale=wb_s[:, m],
+                rhs=g_w[h][:].bitcast(FP8X4), rhs_scale=g_s[h][:], start=True, stop=False,
+            )
+            nc.tensor.matmul_mx(
+                out=bank[:], lhsT=wb8_w[:, m].bitcast(FP8X4), lhsT_scale=wb_s[:, N + P * t : N + P * (t + 1)],
+                rhs=g_w[h][:].bitcast(FP8X4), rhs_scale=g_s[h][:], start=False, stop=False,
+            )
+            nc.tensor.matmul_mx(
+                out=bank[:], lhsT=up_w[:, m].bitcast(FP8X4), lhsT_scale=up_s[:, m],
+                rhs=h_w[h][:].bitcast(FP8X4), rhs_scale=h_s[h][:], start=False, stop=True,
+            )
+            y_sb[(h, t)] = sb([P, HALF], F32, f"y_{h}_{t}")
+            nc.scalar.activation(y_sb[(h, t)][:], bank[:], ACT.Identity, bias=bias1[:, t : t + 1])
+
+        out_rows = out_0.rearrange("(p t) j -> p t j", t=PACK)
+        out_words = out_1[0].rearrange("p j i -> p (j i)").bitcast(I32)
+        o_f = {}
+
+        def cross(h, t, c0, count):
+            nc.vector.tensor_tensor(
+                o_f[h][:, t, c0 : c0 + count], x_t[t][:].indirect(entries(h * HALF + c0, count)),
+                y_sb[(h, t)][:, c0 : c0 + count], ALU.mult,
+            )
+            if c0 + count == HALF:
+                nc.sync.dma_start(out=out_rows[:, t, h * HALF : (h + 1) * HALF], in_=o_f[h][:, t, :])
+
+        for h in range(HALVES):
+            first_stage(h)
+        for t in range(PACK):
+            for h in range(HALVES):
+                second_stage(h, t)
+        for h in range(HALVES):
+            o_f[h] = sb([P, PACK, HALF], F32, f"o_{h}")
+        for t in range(PACK - 1):
+            for h in range(HALVES):
+                cross(h, t, 0, HALF)
+
+        o_s = sb([P, J], U8, "o_s")
+        o_b = []
+        for u in range(J // QU):
+            h, c0 = divmod(u * QU, HALF)
+            cross(h, PACK - 1, c0, QU)
+        for u in range(J // QU):
+            h, c0 = divmod(u * QU, HALF)
+            ob = sb([P, QU * PACK], BF16, f"o_b{u}")
+            weave = nc.vector.tensor_copy if u in (3,) else nc.scalar.copy
+            weave(
+                ob[:].rearrange("p (c i t) -> p c t i", t=PACK, i=4),
+                o_f[h][:, :, c0 : c0 + QU].rearrange("p t (c i) -> p c t i", i=4),
+            )
+            o_b.append(ob)
+        for u in range(J // QU):
+            ow = sb([P, QU], U32, f"o_w{u}")
+            nc.vector.quantize_mx(out=ow[:].bitcast(FP8X4), scales=o_s[:, u * QU : (u + 1) * QU], in_=o_b[u][:])
+            nc.sync.dma_start(out=out_words[:, u * QU : (u + 1) * QU], in_=ow[:].bitcast(I32))
+        for q in range(4):
+            nc.scalar.dma_start(out=out_2[0, 4 * q : 4 * q + 4, :].bitcast(I32), in_=o_s[32 * q : 32 * q + 4, :].bitcast(I32))

@@ -31,17 +31,21 @@ def tile_list_xcross_res_noneP_kernel(
     nc = tc.nc
     with ExitStack() as ctx:
         keep = ctx.enter_context(tc.tile_pool(name="keep", bufs=1))
+        shared = ctx.enter_context(tc.tile_pool(name="shared", bufs=1))
         psum = ctx.enter_context(tc.psum_pool(name="psum", bufs=1))
 
         def sb(shape, dtype, name, tag=""):
             return keep.tile(shape, dtype, name=name, tag=tag or name, align_bytes=64)
 
+        def placed(shape, dtype, name, offset):
+            return shared.tile(shape, dtype, name=name, offset=offset, align_bytes=64)
+
         def load(tile, src):
             nc.sync.dma_start(out=tile.bitcast(I32), in_=src.bitcast(I32))
 
-        def load_scale_rows(queue, tile, rows):
-            for q in range(4):
-                queue.dma_start(out=tile[32 * q : 32 * q + 4, :].bitcast(I32), in_=rows[4 * q : 4 * q + 4, :].bitcast(I32))
+        def load_scale_rows(tile, rows):
+            for r in range(4):
+                load(tile[r:P:32, :], rows[r:16:4, :])
 
         offsets = keep.tile([P, J // 16], U16, name="offsets")
 
@@ -49,8 +53,8 @@ def tile_list_xcross_res_noneP_kernel(
             return offsets[:, start // 16 : (start + count) // 16]
 
         tab_s = sb([P, T], U8, "tab_s")
-        dn_s_raw = sb([P, R], U8, "dn_s_raw", "dn_s_raw_g_w1")
-        wb_s_raw = sb([P, 2 * N], U8, "wb_s_raw", "wb_s_raw_up_b")
+        dn_s_raw = placed([P, R], U8, "dn_s_raw", 256)
+        wb_s_raw = sb([P, 2 * N], U8, "wb_s_raw", "wb_s_raw_h_w0")
         wb_s_rows = sb([16, 2 * N], U8, "wb_s_rows")
         nc.vector.memset(tab_s[:].bitcast(I32), 0)
         nc.vector.memset(dn_s_raw[:].bitcast(I32), 0)
@@ -58,7 +62,7 @@ def tile_list_xcross_res_noneP_kernel(
 
         tab_w = sb([P, T], U32, "tab_w")
         dn_w_raw = sb([P, 2 * R], U8, "dn_w_raw")
-        up_raw = sb([P, PACK, N], F32, "up_raw", "up_raw_h_w0")
+        up_raw = sb([P, PACK, N], F32, "up_raw", "up_raw_bias1")
         wb4_w_raw = sb([P, 2 * N], U8, "wb4_w_raw")
         wb8_w_raw = sb([P, N], U32, "wb8_w_raw")
         bias = sb([P, PACK], F32, "bias")
@@ -67,59 +71,58 @@ def tile_list_xcross_res_noneP_kernel(
 
         nc.gpsimd.dma_start(out=wb_s_rows[:, 0:N].bitcast(I32), in_=wb4_scales[0].bitcast(I32))
         nc.gpsimd.dma_start(out=wb_s_rows[:, N:].bitcast(I32), in_=wb8_scales[0].bitcast(I32))
-        nc.gpsimd.dma_start(out=bias[:], in_=b.rearrange("(p t) -> p t", t=PACK))
-        bias1 = sb([P, PACK], F32, "bias1")
-        nc.gpsimd.tensor_scalar(bias1[:], bias[:], 1.0, 1.0, ALU.mult, ALU.add)
 
+        tab_rows = tab_words[0].rearrange("p t i -> p (t i)")
         nc.sync.dma_start(offsets[:], offs)
+        load(tab_w[:, 0 : T // 2], tab_rows[:, 0 : 2 * T])
+        load_scale_rows(tab_s, tab_scales[0])
+        load(tab_w[:, T // 2 :], tab_rows[:, 2 * T :])
         load(dn_w_raw[:], dn_words[0])
-        load_scale_rows(nc.sync, tab_s, tab_scales[0])
-        load(tab_w[:], tab_words[0].rearrange("p t i -> p (t i)"))
-        load(wb4_w_raw[:], wb4_words[0])
-        load_scale_rows(nc.sync, dn_s_raw, dn_scales[0])
         load(wb8_w_raw[:], wb8_words[0].rearrange("p n i -> p (n i)"))
+        load_scale_rows(dn_s_raw, dn_scales[0])
         nc.sync.dma_start(out=up_raw[:], in_=upw.rearrange("(p i) n -> p i n", i=PACK))
-        load_scale_rows(nc.sync, wb_s_raw, wb_s_rows)
+        load(wb4_w_raw[:], wb4_words[0])
+        load_scale_rows(wb_s_raw, wb_s_rows)
+        nc.sync.dma_start(out=bias[:], in_=b.rearrange("(p t) -> p t", t=PACK))
         for t in range(PACK):
             nc.sync.dma_start(out=x_t[t][:], in_=x_rows[:, t, :])
 
-        g_s = [sb([P, HALF], U8, f"g_s{h}") for h in range(HALVES)]
-        for h in range(HALVES):
-            nc.vector.tensor_copy(g_s[h][:], tab_s[:].indirect(entries(h * HALF, HALF)))
+        g_s = [sb([P, HALF], U8, "g_s0")]
+        nc.vector.tensor_copy(g_s[0][:], tab_s[:].indirect(entries(0, HALF)))
         g_w = [sb([P, HALF], U32, "g_w0")]
-        for c0 in range(0, HALF, QU):
-            nc.vector.tensor_copy(g_w[0][:, c0 : c0 + QU], tab_w[:].indirect(entries(c0, QU)))
+        nc.vector.tensor_copy(g_w[0][:], tab_w[:].indirect(entries(0, HALF)))
         dn_s = sb([P, R], U8, "dn_s")
         nc.vector.tensor_copy(dn_s[:].rearrange("p (t m) -> p t m", t=PACK), dn_s_raw[:].rearrange("p (m t) -> p t m", t=PACK))
-        g_w.append(sb([P, HALF], U32, "g_w1", "dn_s_raw_g_w1"))
+        g_w.append(placed([P, HALF], U32, "g_w1", 512))
         nc.vector.tensor_copy(g_w[1][:], tab_w[:].indirect(entries(HALF, HALF)))
+        g_s.append(placed([P, HALF], U8, "g_s1", 0))
+        nc.vector.tensor_copy(g_s[1][:], tab_s[:].indirect(entries(HALF, HALF)))
 
         def deal_words(dst, src):
             nc.scalar.copy(dst.rearrange("p (t m) -> p t m", t=PACK), src.rearrange("p (m t) -> p t m", t=PACK))
 
         dn_w = sb([P, 2 * R], U8, "dn_w")
         deal_words(dn_w[:].bitcast(U16), dn_w_raw[:].bitcast(U16))
-        wb4_w = sb([P, 2 * N], U8, "wb4_w")
-        deal_words(wb4_w[:].bitcast(U16), wb4_w_raw[:].bitcast(U16))
         wb8_w = sb([P, N], U32, "wb8_w")
         deal_words(wb8_w[:], wb8_w_raw[:])
+        wb4_w = sb([P, 2 * N], U8, "wb4_w")
+        deal_words(wb4_w[:].bitcast(U16), wb4_w_raw[:].bitcast(U16))
 
+        up_b = sb([P, PACK * N], BF16, "up_b")
+        nc.vector.tensor_copy(
+            up_b[:].rearrange("p (t m i) -> p m i t", t=PACK, i=PACK), up_raw[:].rearrange("p i (m t) -> p m i t", t=PACK)
+        )
         wb_s = sb([P, 2 * N], U8, "wb_s")
         nc.vector.tensor_copy(
             wb_s[:].rearrange("p (w t m) -> p w t m", w=2, t=PACK), wb_s_raw[:].rearrange("p (w m t) -> p w t m", w=2, t=PACK)
         )
-        up_b = sb([P, PACK * N], BF16, "up_b", "wb_s_raw_up_b")
-        nc.vector.tensor_copy(
-            up_b[:].rearrange("p (t m i) -> p m i t", t=PACK, i=PACK), up_raw[:].rearrange("p i (m t) -> p m i t", t=PACK)
-        )
-        up_w = sb([P, N], U32, "up_w")
-        up_s = sb([P, N], U8, "up_s")
-        nc.vector.quantize_mx(out=up_w[:].bitcast(FP8X4), scales=up_s[:], in_=up_b[:])
+        bias1 = sb([P, PACK], F32, "bias1", "up_raw_bias1")
+        nc.vector.tensor_scalar(bias1[:], bias[:], 1.0, None, ALU.add)
 
         h_w, h_s, y_sb = {}, {}, {}
 
         def first_stage(h):
-            h_b = sb([P, HALF * PACK], BF16, f"h_b{h}")
+            h_b = sb([P, HALF * PACK], BF16, f"h_b{h}", "h_b0_h_w1" if h == 0 else "")
             for c in range(HALF // CH):
                 bank = psum.tile([P, PACK, CH], F32, name="h_bank", tag=f"bank{h * 4 + c}")
                 cols = slice(c * CH, (c + 1) * CH)
@@ -134,25 +137,25 @@ def tile_list_xcross_res_noneP_kernel(
                     h_b[:, c * CH * PACK : (c + 1) * CH * PACK].rearrange("p (j t) -> p j t", t=PACK),
                     bank[:].rearrange("p t j -> p j t"),
                 )
-            h_w[h] = sb([P, HALF], U32, f"h_w{h}", "up_raw_h_w0" if h == 0 else "")
+            h_w[h] = sb([P, HALF], U32, f"h_w{h}", "wb_s_raw_h_w0" if h == 0 else "h_b0_h_w1")
             h_s[h] = sb([P, HALF], U8, f"h_s{h}")
             nc.vector.quantize_mx(out=h_w[h][:].bitcast(FP8X4), scales=h_s[h][:], in_=h_b[:])
 
         def second_stage(h, t):
             bank = psum.tile([P, HALF], F32, name="y_bank", tag=f"bank{len(y_sb)}")
             m = slice(P * t, P * (t + 1))
-            nc.tensor.matmul_mx(
-                out=bank[:], lhsT=wb4_w[:, 2 * P * t : 2 * P * (t + 1)].bitcast(FP4X4), lhsT_scale=wb_s[:, m],
-                rhs=g_w[h][:].bitcast(FP8X4), rhs_scale=g_s[h][:], start=True, stop=False,
-            )
-            nc.tensor.matmul_mx(
-                out=bank[:], lhsT=wb8_w[:, m].bitcast(FP8X4), lhsT_scale=wb_s[:, N + P * t : N + P * (t + 1)],
-                rhs=g_w[h][:].bitcast(FP8X4), rhs_scale=g_s[h][:], start=False, stop=False,
-            )
-            nc.tensor.matmul_mx(
-                out=bank[:], lhsT=up_w[:, m].bitcast(FP8X4), lhsT_scale=up_s[:, m],
-                rhs=h_w[h][:].bitcast(FP8X4), rhs_scale=h_s[h][:], start=False, stop=True,
-            )
+            passes = [
+                (wb4_w[:, 2 * P * t : 2 * P * (t + 1)].bitcast(FP4X4), wb_s[:, m], g_w[h], g_s[h]),
+                (wb8_w[:, m].bitcast(FP8X4), wb_s[:, N + P * t : N + P * (t + 1)], g_w[h], g_s[h]),
+                (up_w[:, m].bitcast(FP8X4), up_s[:, m], h_w[h], h_s[h]),
+            ]
+            if t > 0:
+                passes = passes[::-1]
+            for n, (w_codes, w_scales, codes, scales) in enumerate(passes):
+                nc.tensor.matmul_mx(
+                    out=bank[:], lhsT=w_codes, lhsT_scale=w_scales, rhs=codes[:].bitcast(FP8X4), rhs_scale=scales[:],
+                    start=(n == 0), stop=(n == len(passes) - 1),
+                )
             y_sb[(h, t)] = sb([P, HALF], F32, f"y_{h}_{t}")
             nc.scalar.activation(y_sb[(h, t)][:], bank[:], ACT.Identity, bias=bias1[:, t : t + 1])
 
@@ -168,16 +171,18 @@ def tile_list_xcross_res_noneP_kernel(
             if c0 + count == HALF:
                 nc.sync.dma_start(out=out_rows[:, t, h * HALF : (h + 1) * HALF], in_=o_f[h][:, t, :])
 
-        for h in range(HALVES):
-            first_stage(h)
-        for t in range(PACK):
-            for h in range(HALVES):
-                second_stage(h, t)
-        for h in range(HALVES):
-            o_f[h] = sb([P, PACK, HALF], F32, f"o_{h}")
-        for t in range(PACK - 1):
-            for h in range(HALVES):
-                cross(h, t, 0, HALF)
+        first_stage(0)
+        up_w = sb([P, N], U32, "up_w")
+        up_s = sb([P, N], U8, "up_s")
+        nc.vector.quantize_mx(out=up_w[:].bitcast(FP8X4), scales=up_s[:], in_=up_b[:])
+        first_stage(1)
+        order = [(h, t) for t in range(PACK) for h in range(HALVES)]
+        for h, t in order:
+            second_stage(h, t)
+        for h, t in order[:6]:
+            if h not in o_f:
+                o_f[h] = sb([P, PACK, HALF], F32, f"o_{h}")
+            cross(h, t, 0, HALF)
 
         o_s = sb([P, J], U8, "o_s")
         o_b = []
@@ -193,9 +198,9 @@ def tile_list_xcross_res_noneP_kernel(
                 o_f[h][:, :, c0 : c0 + QU].rearrange("p t (c i) -> p c t i", i=4),
             )
             o_b.append(ob)
-        for u in range(J // QU):
+        for u in (0, 1, 3, 2):
             ow = sb([P, QU], U32, f"o_w{u}")
             nc.vector.quantize_mx(out=ow[:].bitcast(FP8X4), scales=o_s[:, u * QU : (u + 1) * QU], in_=o_b[u][:])
             nc.sync.dma_start(out=out_words[:, u * QU : (u + 1) * QU], in_=ow[:].bitcast(I32))
-        for q in range(4):
-            nc.scalar.dma_start(out=out_2[0, 4 * q : 4 * q + 4, :].bitcast(I32), in_=o_s[32 * q : 32 * q + 4, :].bitcast(I32))
+        for r in range(4):
+            nc.scalar.dma_start(out=out_2[0, r:16:4, :].bitcast(I32), in_=o_s[r:P:32, :].bitcast(I32))

from contextlib import ExitStack

import concourse.mybir as mybir

K, R, N, T, J = 512, 512, 512, 2048, 1024
FLOPS = 2 * J * (K * R + 2 * K * N + R * N)

F32 = mybir.dt.float32
BF16 = mybir.dt.bfloat16
I32 = mybir.dt.int32
U32 = mybir.dt.uint32
U16 = mybir.dt.uint16
U8 = mybir.dt.uint8
FP8X4 = mybir.dt.float8_e4m3fn_x4
FP4X4 = mybir.dt.float4_e2m1fn_x4
ALU = mybir.AluOpType
ACT = mybir.ActivationFunctionType

P = 128
PACK = 4
HALF = 512
HALVES = J // HALF
CH = 128
QU = 256


def tile_list_xcross_res_noneP_kernel(
    tc, tab_words, tab_scales, wb4_words, wb4_scales, wb8_words, wb8_scales, dn_words, dn_scales, upw, x0T, b, offs,
    out_0, out_1, out_2,
):
    nc = tc.nc
    with ExitStack() as ctx:
        keep = ctx.enter_context(tc.tile_pool(name="keep", bufs=1))
        shared = ctx.enter_context(tc.tile_pool(name="shared", bufs=1))
        psum = ctx.enter_context(tc.psum_pool(name="psum", bufs=1))

        def sb(shape, dtype, name, tag=""):
            return keep.tile(shape, dtype, name=name, tag=tag or name, align_bytes=64)

        def placed(shape, dtype, name, offset):
            return shared.tile(shape, dtype, name=name, offset=offset, align_bytes=64)

        def load(tile, src):
            nc.sync.dma_start(out=tile.bitcast(I32), in_=src.bitcast(I32))

        def load_scale_rows(tile, rows):
            for r in range(4):
                load(tile[r:P:32, :], rows[r:16:4, :])

        offsets = keep.tile([P, J // 16], U16, name="offsets")

        def entries(start, count):
            return offsets[:, start // 16 : (start + count) // 16]

        tab_s = sb([P, T], U8, "tab_s")
        dn_s_raw = placed([P, R], U8, "dn_s_raw", 256)
        wb_s_raw = sb([P, 2 * N], U8, "wb_s_raw", "wb_s_raw_h_w0")
        wb_s_rows = sb([16, 2 * N], U8, "wb_s_rows")
        nc.vector.memset(tab_s[:].bitcast(I32), 0)
        nc.vector.memset(dn_s_raw[:].bitcast(I32), 0)
        nc.vector.memset(wb_s_raw[:].bitcast(I32), 0)

        tab_w = sb([P, T], U32, "tab_w")
        dn_w_raw = sb([P, 2 * R], U8, "dn_w_raw")
        up_raw = sb([P, PACK, N], F32, "up_raw", "up_raw_bias1")
        wb4_w_raw = sb([P, 2 * N], U8, "wb4_w_raw")
        wb8_w_raw = sb([P, N], U32, "wb8_w_raw")
        bias = sb([P, PACK], F32, "bias")
        x_t = [sb([P, T], F32, f"x_{t}") for t in range(PACK)]
        x_rows = x0T.rearrange("(p t) c -> p t c", t=PACK)

        nc.gpsimd.dma_start(out=wb_s_rows[:, 0:N].bitcast(I32), in_=wb4_scales[0].bitcast(I32))
        nc.gpsimd.dma_start(out=wb_s_rows[:, N:].bitcast(I32), in_=wb8_scales[0].bitcast(I32))

        tab_rows = tab_words[0].rearrange("p t i -> p (t i)")
        nc.sync.dma_start(offsets[:], offs)
        load(tab_w[:, 0 : T // 2], tab_rows[:, 0 : 2 * T])
        load_scale_rows(tab_s, tab_scales[0])
        load(tab_w[:, T // 2 :], tab_rows[:, 2 * T :])
        load(dn_w_raw[:], dn_words[0])
        load(wb8_w_raw[:], wb8_words[0].rearrange("p n i -> p (n i)"))
        load_scale_rows(dn_s_raw, dn_scales[0])
        nc.sync.dma_start(out=up_raw[:], in_=upw.rearrange("(p i) n -> p i n", i=PACK))
        load(wb4_w_raw[:], wb4_words[0])
        load_scale_rows(wb_s_raw, wb_s_rows)
        nc.sync.dma_start(out=bias[:], in_=b.rearrange("(p t) -> p t", t=PACK))
        for t in range(PACK):
            nc.sync.dma_start(out=x_t[t][:], in_=x_rows[:, t, :])

        g_s = [sb([P, HALF], U8, "g_s0")]
        nc.vector.tensor_copy(g_s[0][:], tab_s[:].indirect(entries(0, HALF)))
        g_w = [sb([P, HALF], U32, "g_w0")]
        nc.vector.tensor_copy(g_w[0][:], tab_w[:].indirect(entries(0, HALF)))
        dn_s = sb([P, R], U8, "dn_s")
        nc.vector.tensor_copy(dn_s[:].rearrange("p (t m) -> p t m", t=PACK), dn_s_raw[:].rearrange("p (m t) -> p t m", t=PACK))
        g_w.append(placed([P, HALF], U32, "g_w1", 512))
        nc.vector.tensor_copy(g_w[1][:], tab_w[:].indirect(entries(HALF, HALF)))
        g_s.append(placed([P, HALF], U8, "g_s1", 0))
        nc.vector.tensor_copy(g_s[1][:], tab_s[:].indirect(entries(HALF, HALF)))

        def deal_words(dst, src):
            nc.scalar.copy(dst.rearrange("p (t m) -> p t m", t=PACK), src.rearrange("p (m t) -> p t m", t=PACK))

        dn_w = sb([P, 2 * R], U8, "dn_w")
        deal_words(dn_w[:].bitcast(U16), dn_w_raw[:].bitcast(U16))
        wb8_w = sb([P, N], U32, "wb8_w")
        deal_words(wb8_w[:], wb8_w_raw[:])
        wb4_w = sb([P, 2 * N], U8, "wb4_w")
        deal_words(wb4_w[:].bitcast(U16), wb4_w_raw[:].bitcast(U16))

        up_b = sb([P, PACK * N], BF16, "up_b")
        nc.vector.tensor_copy(
            up_b[:].rearrange("p (t m i) -> p m i t", t=PACK, i=PACK), up_raw[:].rearrange("p i (m t) -> p m i t", t=PACK)
        )
        wb_s = sb([P, 2 * N], U8, "wb_s")
        nc.vector.tensor_copy(
            wb_s[:].rearrange("p (w t m) -> p w t m", w=2, t=PACK), wb_s_raw[:].rearrange("p (w m t) -> p w t m", w=2, t=PACK)
        )
        bias1 = sb([P, PACK], F32, "bias1", "up_raw_bias1")
        nc.vector.tensor_scalar(bias1[:], bias[:], 1.0, None, ALU.add)

        h_w, h_s, y_sb = {}, {}, {}

        def first_stage(h):
            h_b = sb([P, HALF * PACK], BF16, f"h_b{h}", "h_b0_h_w1" if h == 0 else "")
            for c in range(HALF // CH):
                bank = psum.tile([P, PACK, CH], F32, name="h_bank", tag=f"bank{h * 4 + c}")
                cols = slice(c * CH, (c + 1) * CH)
                for t in range(PACK):
                    nc.tensor.matmul_mx(
                        out=bank[:, t, :],
                        lhsT=dn_w[:, 2 * P * t : 2 * P * (t + 1)].bitcast(FP4X4), lhsT_scale=dn_s[:, P * t : P * (t + 1)],
                        rhs=g_w[h][:, cols].bitcast(FP8X4), rhs_scale=g_s[h][:, cols],
                        start=True, stop=True,
                    )
                nc.scalar.copy(
                    h_b[:, c * CH * PACK : (c + 1) * CH * PACK].rearrange("p (j t) -> p j t", t=PACK),
                    bank[:].rearrange("p t j -> p j t"),
                )
            h_w[h] = sb([P, HALF], U32, f"h_w{h}", "wb_s_raw_h_w0" if h == 0 else "h_b0_h_w1")
            h_s[h] = sb([P, HALF], U8, f"h_s{h}")
            nc.vector.quantize_mx(out=h_w[h][:].bitcast(FP8X4), scales=h_s[h][:], in_=h_b[:])

        def second_stage(h, t):
            bank = psum.tile([P, HALF], F32, name="y_bank", tag=f"bank{len(y_sb)}")
            m = slice(P * t, P * (t + 1))
            passes = [
                (wb4_w[:, 2 * P * t : 2 * P * (t + 1)].bitcast(FP4X4), wb_s[:, m], g_w[h], g_s[h]),
                (wb8_w[:, m].bitcast(FP8X4), wb_s[:, N + P * t : N + P * (t + 1)], g_w[h], g_s[h]),
                (up_w[:, m].bitcast(FP8X4), up_s[:, m], h_w[h], h_s[h]),
            ]
            if t > 0:
                passes = passes[::-1]
            for n, (w_codes, w_scales, codes, scales) in enumerate(passes):
                nc.tensor.matmul_mx(
                    out=bank[:], lhsT=w_codes, lhsT_scale=w_scales, rhs=codes[:].bitcast(FP8X4), rhs_scale=scales[:],
                    start=(n == 0), stop=(n == len(passes) - 1),
                )
            y_sb[(h, t)] = sb([P, HALF], F32, f"y_{h}_{t}")
            nc.scalar.activation(y_sb[(h, t)][:], bank[:], ACT.Identity, bias=bias1[:, t : t + 1])

        out_rows = out_0.rearrange("(p t) j -> p t j", t=PACK)
        out_words = out_1[0].rearrange("p j i -> p (j i)").bitcast(I32)
        o_f = {}

        def cross(h, t, c0, count):
            nc.vector.tensor_tensor(
                o_f[h][:, t, c0 : c0 + count], x_t[t][:].indirect(entries(h * HALF + c0, count)),
                y_sb[(h, t)][:, c0 : c0 + count], ALU.mult,
            )
            if c0 + count == HALF:
                nc.sync.dma_start(out=out_rows[:, t, h * HALF : (h + 1) * HALF], in_=o_f[h][:, t, :])

        first_stage(0)
        up_w = sb([P, N], U32, "up_w")
        up_s = sb([P, N], U8, "up_s")
        nc.vector.quantize_mx(out=up_w[:].bitcast(FP8X4), scales=up_s[:], in_=up_b[:])
        first_stage(1)
        order = [(h, t) for t in range(PACK) for h in range(HALVES)]
        for h, t in order:
            second_stage(h, t)
        for h, t in order[:6]:
            if h not in o_f:
                o_f[h] = sb([P, PACK, HALF], F32, f"o_{h}")
            cross(h, t, 0, HALF)

        o_s = sb([P, J], U8, "o_s")
        o_b = []
        for u in range(J // QU):
            h, c0 = divmod(u * QU, HALF)
            cross(h, PACK - 1, c0, QU)
        for u in range(J // QU):
            h, c0 = divmod(u * QU, HALF)
            ob = sb([P, QU * PACK], BF16, f"o_b{u}")
            weave = nc.vector.tensor_copy if u in (3,) else nc.scalar.copy
            weave(
                ob[:].rearrange("p (c i t) -> p c t i", t=PACK, i=4),
                o_f[h][:, :, c0 : c0 + QU].rearrange("p t (c i) -> p c t i", i=4),
            )
            o_b.append(ob)
        for u in (0, 1, 3, 2):
            ow = sb([P, QU], U32, f"o_w{u}")
            nc.vector.quantize_mx(out=ow[:].bitcast(FP8X4), scales=o_s[:, u * QU : (u + 1) * QU], in_=o_b[u][:])
            nc.sync.dma_start(out=out_words[:, u * QU : (u + 1) * QU], in_=ow[:].bitcast(I32))
        for r in range(4):
            nc.scalar.dma_start(out=out_2[0, r:16:4, :].bitcast(I32), in_=o_s[r:P:32, :].bitcast(I32))
